import numpy as np
import ml_dtypes


def mxq(x, axis, fmt="e4m3"):
    dtype, down = {"e4m3": (ml_dtypes.float8_e4m3fn, 7), "e5m2": (ml_dtypes.float8_e5m2, 14)}[fmt]
    v = np.moveaxis(np.asarray(x, np.float32).astype(ml_dtypes.bfloat16).astype(np.float64), axis, -1)
    blocks = v.reshape(v.shape[:-1] + (-1, 32))
    amax = np.abs(blocks).max(-1, keepdims=True)
    byte = np.maximum(np.where(amax > 0, np.frexp(amax)[1] - 1 + 127, 0) - down, 1)
    scale = np.exp2(byte - 127.0)
    codes = (blocks / scale).astype(np.float32).astype(dtype).astype(np.float64)
    return np.moveaxis((codes * scale).reshape(v.shape), -1, axis)


WIDE = False


def mx_kscale(k):
    if not WIDE:
        return np.ones(k)
    levels = np.array([30, -30])
    if k % 512:
        return np.exp2(np.random.permutation(np.resize(levels, k // 32))).repeat(32)
    a = np.empty((k // 512, 16))
    for p in range(k // 512):
        a[p, :8] = np.random.permutation(np.resize(levels, 8))
        for g in range(8):
            far = levels[np.abs(levels - a[p, g]) >= 10]
            a[p, g + 8] = far[np.random.randint(len(far))]
    return np.exp2(a.ravel()).repeat(32)


def f64(x):
    return np.asarray(x).astype(np.float64)


def striped(idx):
    return np.tile(np.asarray(idx).reshape(-1, 16).T, (8, 1)).astype(np.uint16)


def unstriped(offs):
    return offs[:16].T.reshape(-1).astype(np.int64)


E2M1 = np.array([0.0, 0.5, 1.0, 1.5, 2.0, 3.0, 4.0, 6.0, -0.0, -0.5, -1.0, -1.5, -2.0, -3.0, -4.0, -6.0])


def pack_weight(w, fmt):
    k, n = w.shape
    w = f64(np.asarray(w, np.float32).astype(ml_dtypes.bfloat16)).reshape(k // 32, 32, n)
    amax = np.abs(w).max(1)
    if fmt == "e4m3":
        byte = np.frexp(amax)[1] - 1 + 127 - 7
    else:
        mant, ex = np.frexp(amax / 6.0)
        byte = np.where(mant > 0.5, ex, ex - 1) + 127
    byte = np.clip(np.where(amax > 0, byte, 1), 1, 254)
    scaled = (w * np.exp2(127.0 - byte)[:, None, :]).reshape(k, n).astype(np.float32)
    by_word = np.ascontiguousarray(scaled.reshape(k // 512, 128, 4, n).transpose(0, 1, 3, 2))
    if fmt == "e4m3":
        words = by_word.astype(ml_dtypes.float8_e4m3fn).view(np.uint8)
    else:
        c = by_word.astype(ml_dtypes.float4_e2m1fn).view(np.uint8) & 0xF
        words = (c[..., 0::2] | (c[..., 1::2] << 4)).reshape(k // 512, 128, 2 * n)
    return np.ascontiguousarray(words), np.ascontiguousarray(byte.astype(np.uint8).reshape(k // 512, 16, n))


def unpack_weight(words, scales, fmt):
    g, _, n = scales.shape
    words = np.ascontiguousarray(words).reshape(g, 128, n, -1)
    if fmt == "e4m3":
        vals = words.view(ml_dtypes.float8_e4m3fn).astype(np.float64)
    else:
        nib = np.empty((g, 128, n, 4), np.uint8)
        nib[..., 0::2] = words & 0xF
        nib[..., 1::2] = words >> 4
        vals = E2M1[nib]
    vals = vals * np.repeat(np.exp2(scales.astype(np.float64) - 127.0), 8, axis=1)[..., None]
    return vals.transpose(0, 1, 3, 2).reshape(g * 512, n)


def sigmoid(v):
    return 1.0 / (1.0 + np.exp(-v))


def sgn(shape):
    return np.random.uniform(0.5, 2.0, shape) * np.where(np.random.standard_normal(shape) < 0, -1.0, 1.0)


K, T, J, R, V, X, O, N, U, E = 512, 1024, 256, 512, 1024, 1024, 256, 256, 128, 512


def setup_inputs():
    n = np.random.standard_normal
    idx = np.random.permutation(V)[:R]
    idx2 = np.random.permutation(T)[:J]
    idx3 = np.random.permutation(X)[:O]
    idx4 = np.random.permutation(X)[:O]
    idx5 = np.random.permutation(J)[:O]
    idx6 = np.random.permutation(O)[:U]
    idx7 = np.random.permutation(E)[:U]
    fk = mx_kscale(K)
    fr = mx_kscale(R)
    xtp = pack_weight(n((K, T)) / fk[:, None], "e2m1")
    wtp = pack_weight(n((K, V)) * 1 / np.sqrt(K) * fk[:, None], "e4m3")
    wbp = pack_weight(n((R, N)) * 1 / np.sqrt(R) / fr[:, None], "e2m1")
    return {
        "xt_words": xtp[0],
        "xt_scales": xtp[1],
        "wt_words": wtp[0],
        "wt_scales": wtp[1],
        "tb": (np.random.randint(-7, 8, (R, X)).astype(np.float64)).astype(np.float32),
        "st": (np.random.uniform(0.15, 0.35, (R, 1)) * fr[:, None]).astype(np.float32),
        "sa": (np.random.uniform(0.5, 1.6, (R, 1)) * fr[:, None]).astype(np.float32),
        "sg": (0.3 * sgn((R, 1))).astype(np.float32),
        "bg": (np.random.uniform(-2.0, 2.0, (R, 1))).astype(np.float32),
        "wb_words": wbp[0],
        "wb_scales": wbp[1],
        "so": (sgn((N, 1))).astype(np.float32),
        "offs": striped(idx),
        "offs2": striped(idx2),
        "offs3": striped(idx3),
        "offs4": striped(idx4),
        "offs5": striped(idx5),
        "offs6": striped(idx6),
        "offs7": striped(idx7),
    }


def reference(xt_words, xt_scales, wt_words, wt_scales, tb, st, sa, sg, bg, wb_words, wb_scales, so, offs, offs2, offs3, offs4, offs5, offs6, offs7):
    idx = unstriped(offs)
    idx2 = unstriped(offs2)
    idx3 = unstriped(offs3)
    idx4 = unstriped(offs4)
    idx5 = unstriped(offs5)
    idx6 = unstriped(offs6)
    idx7 = unstriped(offs7)
    xtu = unpack_weight(xt_words, xt_scales, "e2m1")
    wtu = unpack_weight(wt_words, wt_scales, "e4m3")
    wbu = unpack_weight(wb_words, wb_scales, "e2m1")
    wtidxg = wtu[:, idx]
    xtidx2g = xtu[:, idx2]
    a = wtidxg.T @ xtidx2g
    u1 = f64(tb)[:, idx3] * f64(st) * sigmoid(f64(tb)[:, idx4] * f64(sg) + f64(bg))
    hid = np.maximum(u1, a[:, idx5] * f64(sa))
    hidq = mxq(hid, 0, "e5m2")
    p = wbu.T @ hidq
    m0 = p[:, idx6] * f64(so)
    y = np.zeros((N, E))
    y[:, idx7] = m0
    return y

@@ -1,0 +1,166 @@
+from contextlib import ExitStack
+
+import concourse.mybir as mybir
+
+K, T, J, R, V, X, O, N, U, E = 512, 1024, 256, 512, 1024, 1024, 256, 256, 128, 512
+FLOPS = 2 * K * R * J + 2 * R * N * O
+
+F32 = mybir.dt.float32
+BF16 = mybir.dt.bfloat16
+I32 = mybir.dt.int32
+U32 = mybir.dt.uint32
+U16 = mybir.dt.uint16
+U8 = mybir.dt.uint8
+E4M3X4 = mybir.dt.float8_e4m3fn_x4
+E5M2X4 = mybir.dt.float8_e5m2_x4
+E2M1X4 = mybir.dt.float4_e2m1fn_x4
+ACT = mybir.ActivationFunctionType
+ALU = mybir.AluOpType
+
+P = 128
+PACK = 4
+QUADS = 4
+HALVES = 2
+OH = O // HALVES
+LINE = 4
+
+
+def tile_list_gatedlevels_chosen_one_postedout_kernel(
+    tc, xt_words, xt_scales, wt_words, wt_scales, tb, st, sa, sg, bg, wb_words, wb_scales, so,
+    offs, offs2, offs3, offs4, offs5, offs6, offs7, out,
+):
+    nc = tc.nc
+    with ExitStack() as ctx:
+        sb = ctx.enter_context(tc.tile_pool(name="sb", bufs=1))
+        ps = ctx.enter_context(tc.psum_pool(name="ps", bufs=1))
+
+        def load_list(name, src):
+            tile = sb.tile(list(src.shape), U16, name=name)
+            nc.sync.dma_start(tile[:], src)
+            return tile
+
+        def load_scale_rows(name, src):
+            cols = src.shape[2] // 4
+            tile = sb.tile([PACK, QUADS, cols], I32, name=name)
+            nc.sync.dma_start(tile[:], src[0].bitcast(I32).rearrange("(q r) c -> r q c", r=PACK))
+            return tile
+
+        def load_tb(t):
+            tile = sb.tile([P, X], F32, name="tb%d" % t)
+            nc.sync.dma_start(tile[:], tb.rearrange("(p t) x -> p t x", t=PACK)[:, t, :])
+            return tile
+
+        def per_row(name, src, queue):
+            tile = sb.tile([P, PACK], F32, name=name)
+            queue.dma_start(tile[:], src.rearrange("(p t) one -> p (t one)", t=PACK))
+            return tile
+
+        xs_rows = load_scale_rows("xs_rows", xt_scales)
+        l_tok = load_list("l_tok", offs2)
+        sg_t = per_row("sg_t", sg, nc.scalar)
+        bg_t = per_row("bg_t", bg, nc.scalar)
+        l_gate = load_list("l_gate", offs4)
+        ws_rows = load_scale_rows("ws_rows", wt_scales)
+        xw = sb.tile([P, T], U16, name="xw")
+        nc.sync.dma_start(xw[:].bitcast(I32), xt_words[0].bitcast(I32))
+        tbs = [load_tb(0)]
+        l_level = load_list("l_level", offs3)
+        l_feat = load_list("l_feat", offs)
+        st_t = per_row("st_t", st, nc.sync)
+        ww = sb.tile([P, V], U32, name="ww")
+        nc.sync.dma_start(ww[:].bitcast(I32), wt_words[0].rearrange("p n t -> p (n t)").bitcast(I32))
+        tbs.append(load_tb(1))
+        l_slot = load_list("l_slot", offs5)
+        tbs.extend([load_tb(t) for t in range(2, PACK)])
+        sa_t = per_row("sa_t", sa, nc.sync)
+
+        xs = sb.tile([P, T], U8, name="xs")
+        ws = sb.tile([P, V], U8, name="ws")
+        bs = sb.tile([P, N], U8, name="bs", align_bytes=64)
+        for plane in (xs, ws, bs):
+            nc.vector.memset(plane[:].bitcast(I32), 0)
+        pages = [sb.tile([P, E], F32, name="page%d" % b) for b in range(N // P)]
+        for page in pages:
+            nc.vector.memset(page[:], 0.0)
+
+        bw = sb.tile([P, 2 * N], U8, name="bw", align_bytes=64)
+        nc.sync.dma_start(bw[:].bitcast(I32), wb_words[0].bitcast(I32))
+        for q in range(QUADS):
+            nc.sync.dma_start(bs[32 * q : 32 * q + PACK, :].bitcast(I32), wb_scales[0, PACK * q : PACK * (q + 1), :].bitcast(I32))
+        l_end = load_list("l_end", offs6)
+        l_page = load_list("l_page", offs7)
+        so_t = sb.tile([P, N // P], F32, name="so_t")
+        with nc.allow_non_contiguous_dma(reason="one value a partition"):
+            nc.sync.dma_start(so_t[:], so.rearrange("(b p) one -> p (b one)", p=P))
+
+
+        def spread(plane, rows):
+            for q in range(QUADS):
+                nc.vector.tensor_copy(plane[32 * q : 32 * q + PACK, :].bitcast(I32), rows[:, q, :])
+
+        spread(xs, xs_rows)
+        xs_g = sb.tile([P, J], U8, name="xs_g", align_bytes=64)
+        nc.vector.tensor_copy(xs_g[:], xs[:].indirect(l_tok[:]))
+        xw_g = sb.tile([P, J], U16, name="xw_g", align_bytes=64)
+        nc.vector.tensor_copy(xw_g[:], xw[:].indirect(l_tok[:]))
+        spread(ws, ws_rows)
+        ws_g = sb.tile([P, PACK, P], U8, name="ws_g", align_bytes=64)
+        nc.vector.tensor_copy(ws_g[:].rearrange("p t m -> p m t"), ws[:].indirect(l_feat[:]))
+        ww_g = sb.tile([P, PACK, P], U32, name="ww_g", align_bytes=64)
+        nc.vector.tensor_copy(ww_g[:].rearrange("p t m -> p m t"), ww[:].indirect(l_feat[:]))
+
+        gate = sb.tile([P, PACK, O], F32, name="gate")
+        level = sb.tile([P, PACK, O], F32, name="level")
+        u1 = sb.tile([P, PACK, O], F32, name="u1")
+        for t in range(PACK):
+            nc.scalar.activation(gate[:, t, :], tbs[t][:].indirect(l_gate[:]), ACT.Sigmoid,
+                                 bias=bg_t[:, t : t + 1], scale=sg_t[:, t : t + 1])
+            nc.scalar.activation(level[:, t, :], tbs[t][:].indirect(l_level[:]), ACT.Copy, scale=st_t[:, t : t + 1])
+
+        a_sb = []
+        for t in range(PACK):
+            acc = ps.tile([P, J], F32, name="a_ps%d" % t)
+            nc.tensor.matmul_mx(acc[:], lhsT=ww_g[:, t, :].bitcast(E4M3X4), lhsT_scale=ws_g[:, t, :],
+                                rhs=xw_g[:].bitcast(E2M1X4), rhs_scale=xs_g[:], start=True, stop=True)
+            a_t = sb.tile([P, J], F32, name="a%d" % t)
+            nc.vector.tensor_copy(a_t[:], acc[:])
+            a_sb.append(a_t)
+        for t in range(PACK):
+            nc.vector.tensor_tensor(u1[:, t, :], level[:, t, :], gate[:, t, :], ALU.mult)
+
+        p_sb = [sb.tile([P, O], F32, name="p%d" % b) for b in range(N // P)]
+        for h in range(HALVES):
+            picked = sb.tile([P, PACK, OH], F32, name="picked%d" % h)
+            part = l_slot[:, h * OH // 16 : (h + 1) * OH // 16]
+            for t in range(PACK):
+                nc.scalar.activation(picked[:, t, :], a_sb[t][:].indirect(part), ACT.Copy, scale=sa_t[:, t : t + 1])
+            hid = sb.tile([P, OH, PACK], BF16, name="hid%d" % h, align_bytes=64)
+            nc.vector.tensor_tensor(
+                hid[:].rearrange("p (c i) t -> p c t i", i=LINE),
+                u1[:, :, h * OH : (h + 1) * OH].rearrange("p t (c i) -> p c t i", i=LINE),
+                picked[:].rearrange("p t (c i) -> p c t i", i=LINE),
+                ALU.max,
+            )
+            codes = sb.tile([P, OH], U32, name="codes%d" % h, align_bytes=64)
+            scales = sb.tile([P, OH], U8, name="scales%d" % h, align_bytes=64)
+            nc.vector.quantize_mx(codes[:].bitcast(E5M2X4), scales[:], hid[:].rearrange("p o t -> p (o t)"))
+            for b in range(N // P):
+                acc = ps.tile([P, OH], F32, name="p_ps%d%d" % (h, b))
+                nc.tensor.matmul_mx(acc[:], lhsT=bw[:, 2 * P * b : 2 * P * (b + 1)].bitcast(E2M1X4),
+                                    lhsT_scale=bs[:, P * b : P * (b + 1)],
+                                    rhs=codes[:].bitcast(E5M2X4), rhs_scale=scales[:], start=True, stop=True)
+                dst = p_sb[b][:, h * OH : (h + 1) * OH]
+                if h == HALVES - 1 and b == 0:
+                    nc.scalar.copy(dst, acc[:])
+                else:
+                    nc.vector.tensor_copy(dst, acc[:])
+
+        for b in range(N // P):
+            m0 = sb.tile([P, U], F32, name="m0_%d" % b)
+            nc.scalar.activation(m0[:], p_sb[b][:].indirect(l_end[:]), ACT.Copy, scale=so_t[:, b : b + 1])
+            if b == 0:
+                nc.vector.tensor_copy(pages[b][:].indirect(l_page[:]), m0[:])
+                nc.sync.dma_start(out[P * b : P * (b + 1), :], pages[b][:])
+            else:
+                nc.scalar.activation(pages[b][:].indirect(l_page[:]), m0[:], ACT.Copy)
+                nc.scalar.dma_start(out[P * b : P * (b + 1), :], pages[b][:])

@@ -74,6 +74,11 @@ def tile_list_gatedlevels_chosen_one_postedout_kernel(
         tbs.extend([load_tb(t) for t in range(2, PACK)])
         sa_t = per_row("sa_t", sa, nc.sync)
 
+        warm_in = sb.tile([P, 1], F32, name="warm_in")
+        warm_out = sb.tile([P, 1], F32, name="warm_out")
+        nc.vector.memset(warm_in[:], 0.0)
+        nc.scalar.activation(warm_out[:], warm_in[:], ACT.Sigmoid)
+
         xs = sb.tile([P, T], U8, name="xs")
         ws = sb.tile([P, V], U8, name="ws")
         bs = sb.tile([P, N], U8, name="bs", align_bytes=64)

from contextlib import ExitStack

import concourse.mybir as mybir

K, T, J, R, V, X, O, N, U, E = 512, 1024, 256, 512, 1024, 1024, 256, 256, 128, 512
FLOPS = 2 * K * R * J + 2 * R * N * O

F32 = mybir.dt.float32
BF16 = mybir.dt.bfloat16
I32 = mybir.dt.int32
U32 = mybir.dt.uint32
U16 = mybir.dt.uint16
U8 = mybir.dt.uint8
E4M3X4 = mybir.dt.float8_e4m3fn_x4
E5M2X4 = mybir.dt.float8_e5m2_x4
E2M1X4 = mybir.dt.float4_e2m1fn_x4
ACT = mybir.ActivationFunctionType
ALU = mybir.AluOpType

P = 128
PACK = 4
QUADS = 4
HALVES = 2
OH = O // HALVES
LINE = 4


def tile_list_gatedlevels_chosen_one_postedout_kernel(
    tc, xt_words, xt_scales, wt_words, wt_scales, tb, st, sa, sg, bg, wb_words, wb_scales, so,
    offs, offs2, offs3, offs4, offs5, offs6, offs7, out,
):
    nc = tc.nc
    with ExitStack() as ctx:
        sb = ctx.enter_context(tc.tile_pool(name="sb", bufs=1))
        ps = ctx.enter_context(tc.psum_pool(name="ps", bufs=1))

        def load_list(name, src):
            tile = sb.tile(list(src.shape), U16, name=name)
            nc.sync.dma_start(tile[:], src)
            return tile

        def load_scale_rows(name, src):
            cols = src.shape[2] // 4
            tile = sb.tile([PACK, QUADS, cols], I32, name=name)
            nc.sync.dma_start(tile[:], src[0].bitcast(I32).rearrange("(q r) c -> r q c", r=PACK))
            return tile

        def load_tb(t):
            tile = sb.tile([P, X], F32, name="tb%d" % t)
            nc.sync.dma_start(tile[:], tb.rearrange("(p t) x -> p t x", t=PACK)[:, t, :])
            return tile

        def per_row(name, src, queue):
            tile = sb.tile([P, PACK], F32, name=name)
            queue.dma_start(tile[:], src.rearrange("(p t) one -> p (t one)", t=PACK))
            return tile

        xs_rows = load_scale_rows("xs_rows", xt_scales)
        l_tok = load_list("l_tok", offs2)
        sg_t = per_row("sg_t", sg, nc.scalar)
        bg_t = per_row("bg_t", bg, nc.scalar)
        l_gate = load_list("l_gate", offs4)
        ws_rows = load_scale_rows("ws_rows", wt_scales)
        xw = sb.tile([P, T], U16, name="xw")
        nc.sync.dma_start(xw[:].bitcast(I32), xt_words[0].bitcast(I32))
        tbs = [load_tb(0)]
        l_level = load_list("l_level", offs3)
        l_feat = load_list("l_feat", offs)
        st_t = per_row("st_t", st, nc.sync)
        ww = sb.tile([P, V], U32, name="ww")
        nc.sync.dma_start(ww[:].bitcast(I32), wt_words[0].rearrange("p n t -> p (n t)").bitcast(I32))
        tbs.append(load_tb(1))
        l_slot = load_list("l_slot", offs5)
        tbs.extend([load_tb(t) for t in range(2, PACK)])
        sa_t = per_row("sa_t", sa, nc.sync)

        warm_in = sb.tile([P, 1], F32, name="warm_in")
        warm_out = sb.tile([P, 1], F32, name="warm_out")
        nc.vector.memset(warm_in[:], 0.0)
        nc.scalar.activation(warm_out[:], warm_in[:], ACT.Sigmoid)

        xs = sb.tile([P, T], U8, name="xs")
        ws = sb.tile([P, V], U8, name="ws")
        bs = sb.tile([P, N], U8, name="bs", align_bytes=64)
        for plane in (xs, ws, bs):
            nc.vector.memset(plane[:].bitcast(I32), 0)
        pages = [sb.tile([P, E], F32, name="page%d" % b) for b in range(N // P)]
        for page in pages:
            nc.vector.memset(page[:], 0.0)

        bw = sb.tile([P, 2 * N], U8, name="bw", align_bytes=64)
        nc.sync.dma_start(bw[:].bitcast(I32), wb_words[0].bitcast(I32))
        for q in range(QUADS):
            nc.sync.dma_start(bs[32 * q : 32 * q + PACK, :].bitcast(I32), wb_scales[0, PACK * q : PACK * (q + 1), :].bitcast(I32))
        l_end = load_list("l_end", offs6)
        l_page = load_list("l_page", offs7)
        so_t = sb.tile([P, N // P], F32, name="so_t")
        with nc.allow_non_contiguous_dma(reason="one value a partition"):
            nc.sync.dma_start(so_t[:], so.rearrange("(b p) one -> p (b one)", p=P))


        def spread(plane, rows):
            for q in range(QUADS):
                nc.vector.tensor_copy(plane[32 * q : 32 * q + PACK, :].bitcast(I32), rows[:, q, :])

        spread(xs, xs_rows)
        xs_g = sb.tile([P, J], U8, name="xs_g", align_bytes=64)
        nc.vector.tensor_copy(xs_g[:], xs[:].indirect(l_tok[:]))
        xw_g = sb.tile([P, J], U16, name="xw_g", align_bytes=64)
        nc.vector.tensor_copy(xw_g[:], xw[:].indirect(l_tok[:]))
        spread(ws, ws_rows)
        ws_g = sb.tile([P, PACK, P], U8, name="ws_g", align_bytes=64)
        nc.vector.tensor_copy(ws_g[:].rearrange("p t m -> p m t"), ws[:].indirect(l_feat[:]))
        ww_g = sb.tile([P, PACK, P], U32, name="ww_g", align_bytes=64)
        nc.vector.tensor_copy(ww_g[:].rearrange("p t m -> p m t"), ww[:].indirect(l_feat[:]))

        gate = sb.tile([P, PACK, O], F32, name="gate")
        level = sb.tile([P, PACK, O], F32, name="level")
        u1 = sb.tile([P, PACK, O], F32, name="u1")
        for t in range(PACK):
            nc.scalar.activation(gate[:, t, :], tbs[t][:].indirect(l_gate[:]), ACT.Sigmoid,
                                 bias=bg_t[:, t : t + 1], scale=sg_t[:, t : t + 1])
            nc.scalar.activation(level[:, t, :], tbs[t][:].indirect(l_level[:]), ACT.Copy, scale=st_t[:, t : t + 1])

        a_sb = []
        for t in range(PACK):
            acc = ps.tile([P, J], F32, name="a_ps%d" % t)
            nc.tensor.matmul_mx(acc[:], lhsT=ww_g[:, t, :].bitcast(E4M3X4), lhsT_scale=ws_g[:, t, :],
                                rhs=xw_g[:].bitcast(E2M1X4), rhs_scale=xs_g[:], start=True, stop=True)
            a_t = sb.tile([P, J], F32, name="a%d" % t)
            nc.vector.tensor_copy(a_t[:], acc[:])
            a_sb.append(a_t)
        for t in range(PACK):
            nc.vector.tensor_tensor(u1[:, t, :], level[:, t, :], gate[:, t, :], ALU.mult)

        p_sb = [sb.tile([P, O], F32, name="p%d" % b) for b in range(N // P)]
        for h in range(HALVES):
            picked = sb.tile([P, PACK, OH], F32, name="picked%d" % h)
            part = l_slot[:, h * OH // 16 : (h + 1) * OH // 16]
            for t in range(PACK):
                nc.scalar.activation(picked[:, t, :], a_sb[t][:].indirect(part), ACT.Copy, scale=sa_t[:, t : t + 1])
            hid = sb.tile([P, OH, PACK], BF16, name="hid%d" % h, align_bytes=64)
            nc.vector.tensor_tensor(
                hid[:].rearrange("p (c i) t -> p c t i", i=LINE),
                u1[:, :, h * OH : (h + 1) * OH].rearrange("p t (c i) -> p c t i", i=LINE),
                picked[:].rearrange("p t (c i) -> p c t i", i=LINE),
                ALU.max,
            )
            codes = sb.tile([P, OH], U32, name="codes%d" % h, align_bytes=64)
            scales = sb.tile([P, OH], U8, name="scales%d" % h, align_bytes=64)
            nc.vector.quantize_mx(codes[:].bitcast(E5M2X4), scales[:], hid[:].rearrange("p o t -> p (o t)"))
            for b in range(N // P):
                acc = ps.tile([P, OH], F32, name="p_ps%d%d" % (h, b))
                nc.tensor.matmul_mx(acc[:], lhsT=bw[:, 2 * P * b : 2 * P * (b + 1)].bitcast(E2M1X4),
                                    lhsT_scale=bs[:, P * b : P * (b + 1)],
                                    rhs=codes[:].bitcast(E5M2X4), rhs_scale=scales[:], start=True, stop=True)
                dst = p_sb[b][:, h * OH : (h + 1) * OH]
                if h == HALVES - 1 and b == 0:
                    nc.scalar.copy(dst, acc[:])
                else:
                    nc.vector.tensor_copy(dst, acc[:])

        for b in range(N // P):
            m0 = sb.tile([P, U], F32, name="m0_%d" % b)
            nc.scalar.activation(m0[:], p_sb[b][:].indirect(l_end[:]), ACT.Copy, scale=so_t[:, b : b + 1])
            if b == 0:
                nc.vector.tensor_copy(pages[b][:].indirect(l_page[:]), m0[:])
                nc.sync.dma_start(out[P * b : P * (b + 1), :], pages[b][:])
            else:
                nc.scalar.activation(pages[b][:].indirect(l_page[:]), m0[:], ACT.Copy)
                nc.scalar.dma_start(out[P * b : P * (b + 1), :], pages[b][:])
